import numpy as np
import ml_dtypes


def mxq(x, axis, fmt="e4m3"):
    dtype, down = {"e4m3": (ml_dtypes.float8_e4m3fn, 7), "e5m2": (ml_dtypes.float8_e5m2, 14)}[fmt]
    v = np.moveaxis(np.asarray(x, np.float32).astype(ml_dtypes.bfloat16).astype(np.float64), axis, -1)
    blocks = v.reshape(v.shape[:-1] + (-1, 32))
    amax = np.abs(blocks).max(-1, keepdims=True)
    byte = np.maximum(np.where(amax > 0, np.frexp(amax)[1] - 1 + 127, 0) - down, 1)
    scale = np.exp2(byte - 127.0)
    codes = (blocks / scale).astype(np.float32).astype(dtype).astype(np.float64)
    return np.moveaxis((codes * scale).reshape(v.shape), -1, axis)


WIDE = False


def mx_kscale(k):
    if not WIDE:
        return np.ones(k)
    levels = np.array([10, -10, 5, -5, 0])
    if k % 512:
        return np.exp2(np.random.permutation(np.resize(levels, k // 32))).repeat(32)
    a = np.empty((k // 512, 16))
    for p in range(k // 512):
        a[p, :8] = np.random.permutation(np.resize(levels, 8))
        for g in range(8):
            far = levels[np.abs(levels - a[p, g]) >= 10]
            a[p, g + 8] = far[np.random.randint(len(far))]
    return np.exp2(a.ravel()).repeat(32)


BF16 = ml_dtypes.bfloat16


def bf(x):
    return np.asarray(x, np.float32).astype(BF16)


def f64(x):
    return np.asarray(x).astype(np.float64)


E2M1 = np.array([0.0, 0.5, 1.0, 1.5, 2.0, 3.0, 4.0, 6.0, -0.0, -0.5, -1.0, -1.5, -2.0, -3.0, -4.0, -6.0])


def pack_weight(w, fmt):
    k, n = w.shape
    w = f64(bf(w)).reshape(k // 32, 32, n)
    amax = np.abs(w).max(1)
    if fmt == "e4m3":
        byte = np.frexp(amax)[1] - 1 + 127 - 7
    else:
        mant, ex = np.frexp(amax / 6.0)
        byte = np.where(mant > 0.5, ex, ex - 1) + 127
    byte = np.clip(np.where(amax > 0, byte, 1), 1, 254)
    scaled = (w * np.exp2(127.0 - byte)[:, None, :]).reshape(k, n).astype(np.float32)
    by_word = np.ascontiguousarray(scaled.reshape(k // 512, 128, 4, n).transpose(0, 1, 3, 2))
    if fmt == "e4m3":
        words = by_word.astype(ml_dtypes.float8_e4m3fn).view(np.uint8)
    else:
        c = by_word.astype(ml_dtypes.float4_e2m1fn).view(np.uint8) & 0xF
        words = c[..., 0::2] | (c[..., 1::2] << 4)
    return np.ascontiguousarray(words), np.ascontiguousarray(byte.astype(np.uint8).reshape(k // 512, 16, n))


def unpack_weight(words, scales, fmt):
    g, p, n, _ = words.shape
    if fmt == "e4m3":
        vals = np.ascontiguousarray(words).view(ml_dtypes.float8_e4m3fn).astype(np.float64)
    else:
        nib = np.empty((g, p, n, 4), np.uint8)
        nib[..., 0::2] = words & 0xF
        nib[..., 1::2] = words >> 4
        vals = E2M1[nib]
    vals = vals * np.repeat(np.exp2(scales.astype(np.float64) - 127.0), 8, axis=1)[..., None]
    return vals.transpose(0, 1, 3, 2).reshape(g * 512, n)
def pack4(w):
    words, scales = pack_weight(w, "e2m1")
    return words.reshape(words.shape[0], 128, -1), scales


def unpack4(words, scales):
    return unpack_weight(words.reshape(words.shape[0], 128, -1, 2), scales, "e2m1")


E4M3FN = np.array([(-1.0 if i & 128 else 1.0) * ((1.0 + (i & 7) / 8.0) * 2.0 ** (((i >> 3) & 15) - 7) if i & 120 else (i & 7) * 2.0 ** -9) for i in range(256)])


def e4m3fn_bytes(y):
    return np.clip(np.asarray(y, np.float64), -448.0, 448.0).astype(np.float32).astype(ml_dtypes.float8_e4m3fn).view(np.uint8)


def e4m3fn_values(b):
    return E4M3FN[b]


B, L, K, N, F = 128, 8, 512, 1024, 512


def draw0():
    s, t = mx_kscale(K), mx_kscale(N)
    c = bf(np.random.standard_normal((B, L, K)) * s)
    d_words, d_scales = pack4(np.random.standard_normal((K, N)) / np.sqrt(K) / s[:, None] * t)
    m = bf(np.random.uniform(0.2, 1.0, (L, N)))
    y = bf(np.random.standard_normal((B, N)) * 2.0 * t)
    w_words, w_scales = pack4(np.random.standard_normal((N, F)) / np.sqrt(N) / t[:, None])
    return {
        "c": c,
        "d_words": d_words,
        "d_scales": d_scales,
        "m": m,
        "y": y,
        "w_words": w_words,
        "w_scales": w_scales,
        "thr": bf(np.random.uniform(0.2, 0.6, (F,))),
    }


def gap_project(v, m, y):
    r = y - np.sum(m[None, :, :] * v, axis=1)
    e = np.sum(m * m, axis=0)
    return v + m[None, :, :] * r[:, None, :] / e[None, None, :]


def two_sided_shrink(a, thr):
    return np.maximum(a - thr, 0.0) - np.maximum(-a - thr, 0.0)


def core(c, d_words, d_scales, m, y, w_words, w_scales, thr):
    v = np.matmul(mxq(f64(c), 2, "e4m3"), unpack4(d_words, d_scales))
    x = gap_project(v, f64(m), f64(y))
    a = np.matmul(mxq(x, 2, "e4m3"), unpack4(w_words, w_scales))
    return two_sided_shrink(a, f64(thr))


def setup_inputs():
    drawn = draw0()
    full = np.asarray(drawn['c']).astype(np.float64)
    scale = (np.abs(full).reshape(128, 8, 4, 128).max(axis=(3,)) / 448.0).astype(np.float32)
    given = {}
    for key, value in drawn.items():
        if key == 'c':
            given['c_bytes'] = e4m3fn_bytes(full / np.repeat(scale.astype(np.float64), 128, axis=2))
            given['c_scale'] = scale
        else:
            given[key] = value
    return given


def reference(c_bytes, c_scale, d_words, d_scales, m, y, w_words, w_scales, thr):
    return core(e4m3fn_values(c_bytes) * np.repeat(c_scale.astype(np.float64), 128, axis=2), d_words, d_scales, m, y, w_words, w_scales, thr)

@@ -1,0 +1,406 @@
+from contextlib import ExitStack
+
+import concourse.mybir as mybir
+from concourse.masks import make_identity
+
+B, L, K, N, F = 128, 8, 512, 1024, 512
+P = 128
+T4 = 4
+G = N // 512
+SL = N // P
+FLOPS = 2 * B * L * (K * N + N * F)
+
+F32 = mybir.dt.float32
+BF16 = mybir.dt.bfloat16
+I32 = mybir.dt.int32
+U32 = mybir.dt.uint32
+U8 = mybir.dt.uint8
+FP8 = mybir.dt.float8_e4m3fn
+E4M3X4 = mybir.dt.float8_e4m3fn_x4
+E2M1X4 = mybir.dt.float4_e2m1fn_x4
+
+ALU = mybir.AluOpType
+ACT = mybir.ActivationFunctionType
+ENG = mybir.EngineType
+
+
+def tile_snapshotcompressivegapprojectiondictiona_d1p_kernel(
+    tc, c_bytes, c_scale, d_words, d_scales, m, y, w_words, w_scales, thr, out
+):
+    nc = tc.nc
+    with ExitStack() as ctx:
+        keep = ctx.enter_context(tc.tile_pool(name="keep", bufs=1))
+        work = ctx.enter_context(tc.tile_pool(name="work", bufs=3))
+        psum = ctx.enter_context(tc.psum_pool(name="psum", bufs=1))
+
+        def ktile(shape, dtype, name):
+            return keep.tile(shape, dtype, name=name, tag=name, align_bytes=64)
+
+        def wtile(shape, dtype, tag, bufs):
+            return work.tile(shape, dtype, name=tag, tag=tag, bufs=bufs, align_bytes=64)
+
+        def vbank(h):
+            return psum.tile([P, 512], F32, name="v%d" % h, tag="v%d" % h, bufs=3)
+
+        def tbank():
+            return psum.tile([P, 512], F32, name="tb", tag="tb", bufs=2)
+
+        csc = ktile([P, L * T4], F32, "csc")
+        cby = [ktile([P, 4, K], U8, "cby%d" % j) for j in range(2)]
+        dw_raw = ktile([P, 2 * N], U8, "dw_raw")
+        ds_raw = ktile([P, N], U8, "ds_raw")
+        dw = ktile([P, 2 * N], U8, "dw")
+        ds = ktile([P, N], U8, "ds")
+        ww = ktile([P, G, 2 * F], U8, "ww")
+        ws = ktile([P, G, F], U8, "ws")
+        cst = ktile([P, N], BF16, "cst")
+        tht = ktile([P, P], BF16, "tht")
+        ysb = ktile([P, N], BF16, "ysb")
+        ident = ktile([P, P], F32, "ident")
+
+        nc.vector.memset(ds_raw[:].bitcast(I32), 0)
+        nc.vector.memset(cst[:].bitcast(I32), 0)
+        nc.vector.memset(tht[:].bitcast(I32), 0)
+        nc.vector.memset(ws[:].rearrange("p g f -> p (g f)").bitcast(I32), 0)
+        make_identity(nc, ident[:])
+
+        nc.sync.dma_start(out=csc[:], in_=c_scale.rearrange("b l j -> b (l j)"))
+        for q in range(4):
+            nc.scalar.dma_start(
+                out=ds_raw[32 * q : 32 * q + 4, :].bitcast(I32),
+                in_=d_scales[0, 4 * q : 4 * q + 4, :].bitcast(I32),
+            )
+        for h in range(2):
+            nc.sync.dma_start(out=cby[h][:], in_=c_bytes[:, 4 * h : 4 * h + 4, :])
+        nc.scalar.dma_start(out=dw_raw[:].bitcast(I32), in_=d_words[0].bitcast(I32))
+        nc.gpsimd.dma_start(out=cst[0:L, :], in_=m)
+        nc.gpsimd.dma_start(out=tht[0:4, :], in_=thr.rearrange("(j q) -> j q", q=P))
+        nc.sync.dma_start(out=ysb[:], in_=y)
+        for q in range(4):
+            nc.sync.dma_start(
+                out=ws[32 * q : 32 * q + 4, :, :].bitcast(I32),
+                in_=w_scales[:, 4 * q : 4 * q + 4, :].rearrange("g q n -> q g n").bitcast(I32),
+            )
+        for g in range(G):
+            nc.sync.dma_start(out=ww[:, g, :].bitcast(I32), in_=w_words[g].bitcast(I32))
+
+        cq = ktile([P, B * L], U32, "cq")
+        cs = ktile([P, B * L], U8, "cs")
+        mt = ktile([P, SL, L], F32, "mt")
+        msq = ktile([P, SL, L], F32, "msq")
+        esum = ktile([P, SL], F32, "esum")
+        einv = ktile([P, SL], F32, "einv")
+        tht32 = ktile([P, P], F32, "tht32")
+        thp = ktile([P, 4], F32, "thp")
+        thn = ktile([P, 4], F32, "thn")
+        xb = [ktile([P, T4, L, B], BF16, "xb%d" % g) for g in range(G)]
+        xi = [ktile([P, L, B, T4], BF16, "xi%d" % g) for g in range(G)]
+        xq = [ktile([P, B * L], U32, "xq%d" % g) for g in range(G)]
+        xs = [ktile([P, B * L], U8, "xs%d" % g) for g in range(G)]
+
+        wide = {}
+        grouped = {}
+        cbank = {}
+
+        def widen(l, on_scalar):
+            t = wtile([P, K], BF16, "wide", 4)
+            wide[l] = t
+            for j in range(T4):
+                src = cby[l // 4][:, l % 4, P * j : P * j + P].bitcast(FP8)
+                sc = csc[:, T4 * l + j : T4 * l + j + 1]
+                dst = t[:, P * j : P * j + P]
+                if on_scalar:
+                    nc.scalar.activation(out=dst, in_=src, func=ACT.Copy, scale=sc)
+                else:
+                    nc.vector.tensor_scalar(out=dst, in0=src, scalar1=sc, scalar2=None, op0=ALU.mult)
+
+        def turn(j):
+            bank = vbank(j % 2)
+            cbank[j] = bank
+            for i in range(2):
+                words = wide[2 * j + i][:].bitcast(F32)
+                for u in range(2):
+                    nc.tensor.transpose(
+                        bank[:, 256 * i + 128 * u : 256 * i + 128 * u + 128], words[:, u::2], ident[:]
+                    )
+
+        def regroup(j, on_scalar):
+            gt = wtile([P, 2 * B * T4], BF16, "grouped", 3)
+            grouped[j] = gt
+            dst = gt[:].bitcast(F32).rearrange("p (l b u) -> p l b u", l=2, u=2)
+            src = cbank[j][:].rearrange("p (l u b) -> p l b u", l=2, u=2)
+            if on_scalar:
+                nc.scalar.copy(out=dst, in_=src)
+            else:
+                nc.vector.tensor_copy(out=dst, in_=src)
+
+        def quant_c(j):
+            cols = slice(256 * j, 256 * j + 256)
+            nc.vector.quantize_mx(out=cq[:, cols].bitcast(E4M3X4), scales=cs[:, cols], in_=grouped[j][:])
+
+        def sort_d(g):
+            nc.vector.tensor_copy(
+                out=dw[:, 1024 * g : 1024 * g + 1024].rearrange("p (t q i) -> p t q i", t=4, i=2),
+                in_=dw_raw[:, 1024 * g : 1024 * g + 1024].rearrange("p (q t i) -> p t q i", t=4, i=2),
+            )
+            nc.vector.tensor_copy(
+                out=ds[:, 512 * g : 512 * g + 512].rearrange("p (t q) -> p t q", t=4),
+                in_=ds_raw[:, 512 * g : 512 * g + 512].rearrange("p (q t) -> p t q", t=4),
+            )
+
+        mbank = {}
+
+        def prep_m_turn():
+            bank = tbank()
+            mbank[0] = bank
+            words = cst[:].bitcast(F32)
+            for g in range(G):
+                for u in range(2):
+                    k = 2 * g + u
+                    nc.tensor.transpose(
+                        bank[:, P * k : P * k + P], words[:, 256 * g + u : 256 * (g + 1) : 2], ident[:]
+                    )
+
+        def prep_m():
+            src = mbank[0][:].bitcast(BF16).rearrange("p (k c e) -> p k e c", k=4, e=2)[:, :, :, 0:L]
+            nc.vector.tensor_copy(out=mt[:].rearrange("p (k e) l -> p k e l", e=2), in_=src)
+            nc.vector.tensor_mul(out=msq[:], in0=mt[:], in1=mt[:])
+            nc.vector.tensor_reduce(out=esum[:], in_=msq[:], axis=mybir.AxisListType.X, op=ALU.add)
+            nc.vector.reciprocal(out=einv[:], in_=esum[:])
+
+        def prep_thr():
+            nc.vector.tensor_copy(out=tht32[:], in_=tht[:])
+            bank = tbank()
+            nc.tensor.transpose(bank[:, 0:P], tht32[:], ident[:])
+            nc.vector.tensor_copy(out=thp[:], in_=bank[:, 0:4])
+            nc.vector.tensor_scalar(out=thn[:], in0=thp[:], scalar1=-1.0, scalar2=None, op0=ALU.mult)
+
+        vt = {}
+        st = {}
+        rb = {}
+        rr = {}
+
+        def mm1(s, h):
+            bank = vbank(h)
+            vt[(s, h)] = bank
+            nc.tensor.matmul_mx(
+                out=bank[:],
+                lhsT=dw[:, 256 * s : 256 * s + 256].bitcast(E2M1X4),
+                lhsT_scale=ds[:, P * s : P * s + P],
+                rhs=cq[:, 512 * h : 512 * h + 512].bitcast(E4M3X4),
+                rhs_scale=cs[:, 512 * h : 512 * h + 512],
+                start=True,
+                stop=True,
+            )
+
+        def vcols(s, l):
+            return vt[(s, l // 4)][:, P * (l % 4) : P * (l % 4) + P]
+
+        def weigh(s, ls):
+            for l in ls:
+                if l == 0:
+                    st[s] = tbank()
+                u = wtile([P, P], F32, "u", 12)
+                nc.scalar.activation(out=u[:], in_=vcols(s, l), func=ACT.Copy, scale=mt[:, s, l : l + 1])
+                nc.tensor.matmul(
+                    out=st[s][:, 0:P], lhsT=u[:], rhs=ident[:], start=(l == 0), stop=(l == L - 1), is_transpose=True
+                )
+
+        def resid(s):
+            g, t = s // 4, s % 4
+            r = wtile([P, P], F32, "rbt", 2)
+            rb[s] = r
+            nc.vector.tensor_tensor(
+                out=r[:], in0=ysb[:, 512 * g + t : 512 * (g + 1) : 4], in1=st[s][:, 0:P], op=ALU.subtract
+            )
+
+        def turn_back(s):
+            nc.tensor.transpose(st[s][:, P : 2 * P], rb[s][:], ident[:])
+
+        def scale_back(s):
+            r = wtile([P, P], F32, "rrt", 3)
+            rr[s] = r
+            nc.scalar.activation(out=r[:], in_=st[s][:, P : 2 * P], func=ACT.Copy, scale=einv[:, s : s + 1])
+
+        def project(s, ls):
+            g, t = s // 4, s % 4
+            for l in ls:
+                nc.vector.scalar_tensor_tensor(
+                    out=xb[g][:, t, l, :],
+                    in0=rr[s][:],
+                    scalar=mt[:, s, l : l + 1],
+                    in1=vcols(s, l),
+                    op0=ALU.mult,
+                    op1=ALU.add,
+                )
+
+        def interleave(g, j, on_scalar):
+            dst = xi[g][:, 2 * j : 2 * j + 2, :, :].rearrange("p l b t -> p (l b) t")
+            src = xb[g][:, :, 2 * j : 2 * j + 2, :].rearrange("p t l b -> p (l b) t")
+            if on_scalar:
+                nc.scalar.copy(out=dst, in_=src)
+            else:
+                nc.vector.tensor_copy(out=dst, in_=src)
+
+        def quant_x(g, h):
+            cols = slice(512 * h, 512 * h + 512)
+            nc.vector.quantize_mx(
+                out=xq[g][:, cols].bitcast(E4M3X4),
+                scales=xs[g][:, cols],
+                in_=xi[g][:, 4 * h : 4 * h + 4, :, :].rearrange("p l b t -> p (l b t)"),
+            )
+
+        at = {}
+        res = {}
+
+        def mm2(h, ft, g):
+            if g == 0:
+                at[(h, ft)] = vbank(ft % 2)
+            nc.tensor.matmul_mx(
+                out=at[(h, ft)][:],
+                lhsT=ww[:, g, 256 * ft : 256 * ft + 256].bitcast(E2M1X4),
+                lhsT_scale=ws[:, g, P * ft : P * ft + P],
+                rhs=xq[g][:, 512 * h : 512 * h + 512].bitcast(E4M3X4),
+                rhs_scale=xs[g][:, 512 * h : 512 * h + 512],
+                start=(g == 0),
+                stop=(g == G - 1),
+            )
+
+        def pos_part(h, ft):
+            p = wtile([P, 512], F32, "pos", 6)
+            nc.scalar.activation(out=p[:], in_=at[(h, ft)][:], func=ACT.Relu, bias=thn[:, ft : ft + 1])
+            res.setdefault((h, ft), []).append(p)
+
+        def neg_part(h, ft):
+            q = wtile([P, 512], F32, "neg", 6)
+            nc.vector.tensor_scalar(
+                out=q[:], in0=at[(h, ft)][:], scalar1=thp[:, ft : ft + 1], scalar2=0.0, op0=ALU.add, op1=ALU.min
+            )
+            res.setdefault((h, ft), []).append(q)
+
+        low = {}
+
+        def low_part(h, ft):
+            q = wtile([P, 512], F32, "low", 3)
+            nc.vector.tensor_scalar(
+                out=q[:], in0=at[(h, ft)][:], scalar1=thn[:, ft : ft + 1], scalar2=None, op0=ALU.min
+            )
+            low[(h, ft)] = q
+
+        def both_parts(h, ft):
+            o = wtile([P, 512], F32, "both", 6)
+            nc.vector.scalar_tensor_tensor(
+                out=o[:], in0=at[(h, ft)][:], scalar=thp[:, ft : ft + 1], in1=low[(h, ft)][:], op0=ALU.max, op1=ALU.add
+            )
+            res[(h, ft)] = [o]
+
+        def emit(h, i, on_scalar):
+            l = 4 * h + i
+            bank = tbank() if h == 0 else vbank(i % 2)
+            for ft in range(4):
+                parts = res[(h, ft)]
+                for n, part in enumerate(parts):
+                    nc.tensor.matmul(
+                        out=bank[:, P * ft : P * ft + P],
+                        lhsT=part[:, P * i : P * i + P],
+                        rhs=ident[:],
+                        start=(n == 0),
+                        stop=(n == len(parts) - 1),
+                        is_transpose=True,
+                    )
+            o = wtile([P, F], F32, "o", 6)
+            if on_scalar:
+                nc.scalar.copy(out=o[:], in_=bank[:])
+            else:
+                nc.vector.tensor_copy(out=o[:], in_=bank[:])
+            nc.sync.dma_start(out=out[:, l, :], in_=o[:])
+
+        with tc.manual_schedule(engines={ENG.PE, ENG.Activation, ENG.DVE}):
+            for l in range(L):
+                widen(l, l % 2 == 0)
+            turn(0)
+            turn(1)
+            prep_m_turn()
+            regroup(0, False)
+            regroup(1, True)
+            turn(2)
+            turn(3)
+            quant_c(0)
+            sort_d(0)
+            quant_c(1)
+            mm1(0, 0)
+            regroup(2, True)
+            regroup(3, False)
+            quant_c(2)
+            prep_m()
+            quant_c(3)
+            mm1(0, 1)
+            mm1(1, 0)
+            mm1(1, 1)
+            sort_d(1)
+
+            lo, hi = range(0, 4), range(4, 8)
+            for i in range(SL):
+                weigh(i, range(0, 6))
+                if i > 0:
+                    turn_back(i - 1)
+                weigh(i, range(6, 8))
+                if i == 1:
+                    prep_thr()
+                if i == 5:
+                    interleave(0, 0, True)
+                if i == 6:
+                    interleave(0, 2, True)
+                if i > 0:
+                    scale_back(i - 1)
+                resid(i)
+                if i > 0:
+                    project(i - 1, lo)
+                    project(i - 1, hi)
+                for h in range(2):
+                    if 1 <= i and i + 1 < SL:
+                        mm1(i + 1, h)
+                if i == 4:
+                    interleave(0, 1, False)
+                if i == 6:
+                    quant_x(0, 0)
+            i = SL - 1
+            turn_back(i)
+            interleave(0, 3, False)
+            quant_x(0, 1)
+            scale_back(i)
+            for ft in range(4):
+                mm2(0, ft, 0)
+            for ft in range(2):
+                mm2(1, ft, 0)
+            project(i, lo)
+            interleave(1, 1, True)
+            interleave(1, 0, False)
+            project(i, hi)
+            quant_x(1, 0)
+            interleave(1, 3, True)
+            interleave(1, 2, False)
+            for ft in range(4):
+                mm2(0, ft, 1)
+            quant_x(1, 1)
+            low_part(0, 1)
+            pos_part(0, 0)
+            low_part(0, 3)
+            pos_part(0, 2)
+            both_parts(0, 1)
+            neg_part(0, 0)
+            both_parts(0, 3)
+            neg_part(0, 2)
+            for ft in range(2):
+                mm2(1, ft, 1)
+            for ft in range(2, 4):
+                mm2(1, ft, 0)
+                mm2(1, ft, 1)
+            for ft in range(4):
+                pos_part(1, ft)
+            for ft in range(4):
+                neg_part(1, ft)
+            for ft in range(4):
+                emit(0, ft, True)
+            for i in range(4):
+                emit(1, i, i % 2 == 1)

@@ -4,11 +4,15 @@ import concourse.mybir as mybir
 from concourse.masks import make_identity
 
 B, L, K, N, F = 128, 8, 512, 1024, 512
-P = 128
-T4 = 4
-G = N // 512
-SL = N // P
 FLOPS = 2 * B * L * (K * N + N * F)
+
+P = 128
+T = 4
+G = N // (P * T)
+S = N // P
+FT = F // P
+HF = L // 2
+HALF = HF * B
 
 F32 = mybir.dt.float32
 BF16 = mybir.dt.bfloat16
@@ -23,6 +27,12 @@ ALU = mybir.AluOpType
 ACT = mybir.ActivationFunctionType
 ENG = mybir.EngineType
 
+LOAD_FRAMES = (2, 2, 4)
+
+ON_VECTOR = ((0, 0), (1, 2))
+
+WARM_UPS = 7
+
 
 def tile_snapshotcompressivegapprojectiondictiona_d1p_kernel(
     tc, c_bytes, c_scale, d_words, d_scales, m, y, w_words, w_scales, thr, out
@@ -30,377 +40,408 @@ def tile_snapshotcompressivegapprojectiondictiona_d1p_kernel(
     nc = tc.nc
     with ExitStack() as ctx:
         keep = ctx.enter_context(tc.tile_pool(name="keep", bufs=1))
-        work = ctx.enter_context(tc.tile_pool(name="work", bufs=3))
+        work = ctx.enter_context(tc.tile_pool(name="work", bufs=1))
         psum = ctx.enter_context(tc.psum_pool(name="psum", bufs=1))
 
-        def ktile(shape, dtype, name):
+        def kept(shape, dtype, name):
             return keep.tile(shape, dtype, name=name, tag=name, align_bytes=64)
 
-        def wtile(shape, dtype, tag, bufs):
-            return work.tile(shape, dtype, name=tag, tag=tag, bufs=bufs, align_bytes=64)
+        def rotating(shape, dtype, name, bufs):
+            return work.tile(shape, dtype, name=name, tag=name, bufs=bufs, align_bytes=64)
 
-        def vbank(h):
-            return psum.tile([P, 512], F32, name="v%d" % h, tag="v%d" % h, bufs=3)
+        def product_bank(h):
+            return psum.tile([P, HALF], F32, name="product%d" % h, tag="product%d" % h, bufs=3)
 
-        def tbank():
-            return psum.tile([P, 512], F32, name="tb", tag="tb", bufs=2)
+        def turn_bank():
+            return psum.tile([P, 512], F32, name="turn", tag="turn", bufs=2)
 
-        csc = ktile([P, L * T4], F32, "csc")
-        cby = [ktile([P, 4, K], U8, "cby%d" % j) for j in range(2)]
-        dw_raw = ktile([P, 2 * N], U8, "dw_raw")
-        ds_raw = ktile([P, N], U8, "ds_raw")
-        dw = ktile([P, 2 * N], U8, "dw")
-        ds = ktile([P, N], U8, "ds")
-        ww = ktile([P, G, 2 * F], U8, "ww")
-        ws = ktile([P, G, F], U8, "ws")
-        cst = ktile([P, N], BF16, "cst")
-        tht = ktile([P, P], BF16, "tht")
-        ysb = ktile([P, N], BF16, "ysb")
-        ident = ktile([P, P], F32, "ident")
+        scale_c = kept([P, L * T], F32, "scale_c")
+        bytes_c = [kept([P, frames, K], U8, "bytes_c%d" % j) for j, frames in enumerate(LOAD_FRAMES)]
+        d_in = kept([P, 2 * N], U8, "d_in")
+        d_in_scales = kept([P, N], U8, "d_in_scales")
+        w_in = kept([P, G, 2 * F], U8, "w_in")
+        w_in_scales = kept([P, G, F], U8, "w_in_scales")
+        m_rows = kept([P, N], BF16, "m_rows")
+        thr_rows = kept([P, P], BF16, "thr_rows")
+        y_in = kept([P, N], BF16, "y_in")
+        ident = kept([P, P], F32, "ident")
+        blank = kept([P, 512], BF16, "blank")
 
-        nc.vector.memset(ds_raw[:].bitcast(I32), 0)
-        nc.vector.memset(cst[:].bitcast(I32), 0)
-        nc.vector.memset(tht[:].bitcast(I32), 0)
-        nc.vector.memset(ws[:].rearrange("p g f -> p (g f)").bitcast(I32), 0)
+        nc.vector.memset(d_in_scales[:].bitcast(I32), 0)
+        nc.vector.memset(m_rows[:].bitcast(I32), 0)
+        nc.vector.memset(thr_rows[:].bitcast(I32), 0)
+        nc.vector.memset(w_in_scales[:].rearrange("p g f -> p (g f)").bitcast(I32), 0)
         make_identity(nc, ident[:])
+        nc.vector.memset(blank[:].bitcast(I32), 0)
 
-        nc.sync.dma_start(out=csc[:], in_=c_scale.rearrange("b l j -> b (l j)"))
+        nc.sync.dma_start(out=scale_c[:], in_=c_scale.rearrange("b l j -> b (l j)"))
+        source_c = {}
+        first = 0
+        for j, frames in enumerate(LOAD_FRAMES):
+            nc.sync.dma_start(out=bytes_c[j][:], in_=c_bytes[:, first : first + frames, :])
+            for i in range(frames):
+                source_c[first + i] = (bytes_c[j], i)
+            first += frames
+        nc.scalar.dma_start(out=d_in[:].bitcast(I32), in_=d_words[0].bitcast(I32))
         for q in range(4):
             nc.scalar.dma_start(
-                out=ds_raw[32 * q : 32 * q + 4, :].bitcast(I32),
+                out=d_in_scales[32 * q : 32 * q + 4, :].bitcast(I32),
                 in_=d_scales[0, 4 * q : 4 * q + 4, :].bitcast(I32),
             )
-        for h in range(2):
-            nc.sync.dma_start(out=cby[h][:], in_=c_bytes[:, 4 * h : 4 * h + 4, :])
-        nc.scalar.dma_start(out=dw_raw[:].bitcast(I32), in_=d_words[0].bitcast(I32))
-        nc.gpsimd.dma_start(out=cst[0:L, :], in_=m)
-        nc.gpsimd.dma_start(out=tht[0:4, :], in_=thr.rearrange("(j q) -> j q", q=P))
-        nc.sync.dma_start(out=ysb[:], in_=y)
+        nc.gpsimd.dma_start(out=m_rows[0:L, :], in_=m)
+        nc.gpsimd.dma_start(out=thr_rows[0:FT, :], in_=thr.rearrange("(j q) -> j q", q=P))
+        nc.sync.dma_start(out=y_in[:], in_=y)
         for q in range(4):
             nc.sync.dma_start(
-                out=ws[32 * q : 32 * q + 4, :, :].bitcast(I32),
+                out=w_in_scales[32 * q : 32 * q + 4, :, :].bitcast(I32),
                 in_=w_scales[:, 4 * q : 4 * q + 4, :].rearrange("g q n -> q g n").bitcast(I32),
             )
         for g in range(G):
-            nc.sync.dma_start(out=ww[:, g, :].bitcast(I32), in_=w_words[g].bitcast(I32))
+            nc.sync.dma_start(out=w_in[:, g, :].bitcast(I32), in_=w_words[g].bitcast(I32))
 
-        cq = ktile([P, B * L], U32, "cq")
-        cs = ktile([P, B * L], U8, "cs")
-        mt = ktile([P, SL, L], F32, "mt")
-        msq = ktile([P, SL, L], F32, "msq")
-        esum = ktile([P, SL], F32, "esum")
-        einv = ktile([P, SL], F32, "einv")
-        tht32 = ktile([P, P], F32, "tht32")
-        thp = ktile([P, 4], F32, "thp")
-        thn = ktile([P, 4], F32, "thn")
-        xb = [ktile([P, T4, L, B], BF16, "xb%d" % g) for g in range(G)]
-        xi = [ktile([P, L, B, T4], BF16, "xi%d" % g) for g in range(G)]
-        xq = [ktile([P, B * L], U32, "xq%d" % g) for g in range(G)]
-        xs = [ktile([P, B * L], U8, "xs%d" % g) for g in range(G)]
+        d_codes = kept([P, 2 * N], U8, "d_codes")
+        d_code_scales = kept([P, N], U8, "d_code_scales")
+        c_codes = kept([P, B * L], U32, "c_codes")
+        c_code_scales = kept([P, B * L], U8, "c_code_scales")
+        m_col = kept([P, S, L], F32, "m_col")
+        m_sq = kept([P, S, L], F32, "m_sq")
+        e_sum = kept([P, S], F32, "e_sum")
+        e_inv = kept([P, S], F32, "e_inv")
+        thr_f32 = kept([P, P], F32, "thr_f32")
+        thr_col = kept([P, FT], F32, "thr_col")
+        thr_neg = kept([P, FT], F32, "thr_neg")
+        x_flat = [kept([P, T, L, B], BF16, "x_flat%d" % g) for g in range(G)]
+        x_word = [kept([P, L, B, T], BF16, "x_word%d" % g) for g in range(G)]
+        x_codes = [kept([P, B * L], U32, "x_codes%d" % g) for g in range(G)]
+        x_code_scales = [kept([P, B * L], U8, "x_code_scales%d" % g) for g in range(G)]
 
-        wide = {}
-        grouped = {}
-        cbank = {}
+        def warm_up():
+            bank = product_bank(0)
+            nc.tensor.matmul(out=bank[:], lhsT=blank[:, 0:P], rhs=blank[:], start=True, stop=True)
+
+        c_rows = {}
+        c_turned = {}
+        c_word = {}
 
         def widen(l, on_scalar):
-            t = wtile([P, K], BF16, "wide", 4)
-            wide[l] = t
-            for j in range(T4):
-                src = cby[l // 4][:, l % 4, P * j : P * j + P].bitcast(FP8)
-                sc = csc[:, T4 * l + j : T4 * l + j + 1]
-                dst = t[:, P * j : P * j + P]
+            rows = rotating([P, K], BF16, "c_rows", 8)
+            c_rows[l] = rows
+            tile, i = source_c[l]
+            for j in range(T):
+                source = tile[:, i, P * j : P * j + P].bitcast(FP8)
+                scale = scale_c[:, T * l + j : T * l + j + 1]
+                target = rows[:, P * j : P * j + P]
                 if on_scalar:
-                    nc.scalar.activation(out=dst, in_=src, func=ACT.Copy, scale=sc)
+                    nc.scalar.activation(out=target, in_=source, func=ACT.Copy, scale=scale)
                 else:
-                    nc.vector.tensor_scalar(out=dst, in0=src, scalar1=sc, scalar2=None, op0=ALU.mult)
+                    nc.vector.tensor_scalar(out=target, in0=source, scalar1=scale, scalar2=None, op0=ALU.mult)
 
-        def turn(j):
-            bank = vbank(j % 2)
-            cbank[j] = bank
+        def turn_c(j):
+            bank = product_bank(j % 2)
+            c_turned[j] = bank
             for i in range(2):
-                words = wide[2 * j + i][:].bitcast(F32)
+                words = c_rows[2 * j + i][:].bitcast(F32)
                 for u in range(2):
-                    nc.tensor.transpose(
-                        bank[:, 256 * i + 128 * u : 256 * i + 128 * u + 128], words[:, u::2], ident[:]
-                    )
+                    first = 2 * P * i + P * u
+                    nc.tensor.transpose(bank[:, first : first + P], words[:, u::2], ident[:])
 
-        def regroup(j, on_scalar):
-            gt = wtile([P, 2 * B * T4], BF16, "grouped", 3)
-            grouped[j] = gt
-            dst = gt[:].bitcast(F32).rearrange("p (l b u) -> p l b u", l=2, u=2)
-            src = cbank[j][:].rearrange("p (l u b) -> p l b u", l=2, u=2)
+        def gather_c(j, on_scalar):
+            tile = rotating([P, 2 * B * T], BF16, "c_word", 4)
+            c_word[j] = tile
+            target = tile[:].bitcast(F32).rearrange("p (l b u) -> p l b u", l=2, u=2)
+            source = c_turned[j][:].rearrange("p (l u b) -> p l b u", l=2, u=2)
             if on_scalar:
-                nc.scalar.copy(out=dst, in_=src)
+                nc.scalar.copy(out=target, in_=source)
             else:
-                nc.vector.tensor_copy(out=dst, in_=src)
+                nc.vector.tensor_copy(out=target, in_=source)
 
-        def quant_c(j):
-            cols = slice(256 * j, 256 * j + 256)
-            nc.vector.quantize_mx(out=cq[:, cols].bitcast(E4M3X4), scales=cs[:, cols], in_=grouped[j][:])
+        def quantise_c(j):
+            cols = slice(2 * B * j, 2 * B * (j + 1))
+            nc.vector.quantize_mx(
+                out=c_codes[:, cols].bitcast(E4M3X4), scales=c_code_scales[:, cols], in_=c_word[j][:]
+            )
 
         def sort_d(g):
+            words = slice(1024 * g, 1024 * (g + 1))
             nc.vector.tensor_copy(
-                out=dw[:, 1024 * g : 1024 * g + 1024].rearrange("p (t q i) -> p t q i", t=4, i=2),
-                in_=dw_raw[:, 1024 * g : 1024 * g + 1024].rearrange("p (q t i) -> p t q i", t=4, i=2),
+                out=d_codes[:, words].rearrange("p (t q i) -> p t q i", t=T, i=2),
+                in_=d_in[:, words].rearrange("p (q t i) -> p t q i", t=T, i=2),
             )
+            cols = slice(512 * g, 512 * (g + 1))
             nc.vector.tensor_copy(
-                out=ds[:, 512 * g : 512 * g + 512].rearrange("p (t q) -> p t q", t=4),
-                in_=ds_raw[:, 512 * g : 512 * g + 512].rearrange("p (q t) -> p t q", t=4),
+                out=d_code_scales[:, cols].rearrange("p (t q) -> p t q", t=T),
+                in_=d_in_scales[:, cols].rearrange("p (q t) -> p t q", t=T),
             )
 
-        mbank = {}
+        m_turned = {}
 
-        def prep_m_turn():
-            bank = tbank()
-            mbank[0] = bank
-            words = cst[:].bitcast(F32)
+        def turn_m():
+            bank = turn_bank()
+            m_turned[0] = bank
+            words = m_rows[:].bitcast(F32)
             for g in range(G):
                 for u in range(2):
-                    k = 2 * g + u
+                    first = P * (2 * g + u)
                     nc.tensor.transpose(
-                        bank[:, P * k : P * k + P], words[:, 256 * g + u : 256 * (g + 1) : 2], ident[:]
+                        bank[:, first : first + P], words[:, 256 * g + u : 256 * (g + 1) : 2], ident[:]
                     )
 
-        def prep_m():
-            src = mbank[0][:].bitcast(BF16).rearrange("p (k c e) -> p k e c", k=4, e=2)[:, :, :, 0:L]
-            nc.vector.tensor_copy(out=mt[:].rearrange("p (k e) l -> p k e l", e=2), in_=src)
-            nc.vector.tensor_mul(out=msq[:], in0=mt[:], in1=mt[:])
-            nc.vector.tensor_reduce(out=esum[:], in_=msq[:], axis=mybir.AxisListType.X, op=ALU.add)
-            nc.vector.reciprocal(out=einv[:], in_=esum[:])
+        def prepare_m():
+            source = m_turned[0][:].bitcast(BF16).rearrange("p (k c e) -> p k e c", k=4, e=2)[:, :, :, 0:L]
+            nc.vector.tensor_copy(out=m_col[:].rearrange("p (k e) l -> p k e l", e=2), in_=source)
+            nc.vector.tensor_mul(out=m_sq[:], in0=m_col[:], in1=m_col[:])
+            nc.vector.tensor_reduce(out=e_sum[:], in_=m_sq[:], axis=mybir.AxisListType.X, op=ALU.add)
+            nc.vector.reciprocal(out=e_inv[:], in_=e_sum[:])
 
-        def prep_thr():
-            nc.vector.tensor_copy(out=tht32[:], in_=tht[:])
-            bank = tbank()
-            nc.tensor.transpose(bank[:, 0:P], tht32[:], ident[:])
-            nc.vector.tensor_copy(out=thp[:], in_=bank[:, 0:4])
-            nc.vector.tensor_scalar(out=thn[:], in0=thp[:], scalar1=-1.0, scalar2=None, op0=ALU.mult)
+        def prepare_thr():
+            nc.vector.tensor_copy(out=thr_f32[:], in_=thr_rows[:])
+            bank = turn_bank()
+            nc.tensor.transpose(bank[:, 0:P], thr_f32[:], ident[:])
+            nc.vector.tensor_copy(out=thr_col[:], in_=bank[:, 0:FT])
+            nc.vector.tensor_scalar(out=thr_neg[:], in0=thr_col[:], scalar1=-1.0, scalar2=None, op0=ALU.mult)
 
-        vt = {}
-        st = {}
-        rb = {}
-        rr = {}
+        v_bank = {}
+        weighted = {}
+        sum_bank = {}
+        r_rows = {}
+        r_col = {}
 
-        def mm1(s, h):
-            bank = vbank(h)
-            vt[(s, h)] = bank
+        def multiply_d(s, h):
+            bank = product_bank(h)
+            v_bank[(s, h)] = bank
+            cols = slice(HALF * h, HALF * (h + 1))
             nc.tensor.matmul_mx(
                 out=bank[:],
-                lhsT=dw[:, 256 * s : 256 * s + 256].bitcast(E2M1X4),
-                lhsT_scale=ds[:, P * s : P * s + P],
-                rhs=cq[:, 512 * h : 512 * h + 512].bitcast(E4M3X4),
-                rhs_scale=cs[:, 512 * h : 512 * h + 512],
+                lhsT=d_codes[:, 2 * P * s : 2 * P * (s + 1)].bitcast(E2M1X4),
+                lhsT_scale=d_code_scales[:, P * s : P * (s + 1)],
+                rhs=c_codes[:, cols].bitcast(E4M3X4),
+                rhs_scale=c_code_scales[:, cols],
                 start=True,
                 stop=True,
             )
 
-        def vcols(s, l):
-            return vt[(s, l // 4)][:, P * (l % 4) : P * (l % 4) + P]
+        def v_frame(s, l):
+            first = B * (l % HF)
+            return v_bank[(s, l // HF)][:, first : first + B]
 
-        def weigh(s, ls):
-            for l in ls:
-                if l == 0:
-                    st[s] = tbank()
-                u = wtile([P, P], F32, "u", 12)
-                nc.scalar.activation(out=u[:], in_=vcols(s, l), func=ACT.Copy, scale=mt[:, s, l : l + 1])
-                nc.tensor.matmul(
-                    out=st[s][:, 0:P], lhsT=u[:], rhs=ident[:], start=(l == 0), stop=(l == L - 1), is_transpose=True
-                )
+        def weigh(s, l):
+            tile = rotating([P, B], F32, "weighted", 16)
+            nc.scalar.activation(out=tile[:], in_=v_frame(s, l), func=ACT.Copy, scale=m_col[:, s, l : l + 1])
+            if l == 0:
+                sum_bank[s] = turn_bank()
+            nc.tensor.matmul(
+                out=sum_bank[s][:, 0:P],
+                lhsT=tile[:],
+                rhs=ident[:],
+                start=(l == 0),
+                stop=(l == L - 1),
+                is_transpose=True,
+            )
 
-        def resid(s):
-            g, t = s // 4, s % 4
-            r = wtile([P, P], F32, "rbt", 2)
-            rb[s] = r
+        def residual(s):
+            g, t = s // T, s % T
+            tile = rotating([P, P], F32, "r_rows", 2)
+            r_rows[s] = tile
             nc.vector.tensor_tensor(
-                out=r[:], in0=ysb[:, 512 * g + t : 512 * (g + 1) : 4], in1=st[s][:, 0:P], op=ALU.subtract
+                out=tile[:],
+                in0=y_in[:, 512 * g + t : 512 * (g + 1) : T],
+                in1=sum_bank[s][:, 0:P],
+                op=ALU.subtract,
             )
 
-        def turn_back(s):
-            nc.tensor.transpose(st[s][:, P : 2 * P], rb[s][:], ident[:])
+        def turn_residual(s):
+            nc.tensor.transpose(sum_bank[s][:, P : 2 * P], r_rows[s][:], ident[:])
 
-        def scale_back(s):
-            r = wtile([P, P], F32, "rrt", 3)
-            rr[s] = r
-            nc.scalar.activation(out=r[:], in_=st[s][:, P : 2 * P], func=ACT.Copy, scale=einv[:, s : s + 1])
+        def scale_residual(s):
+            tile = rotating([P, B], F32, "r_col", 6)
+            r_col[s] = tile
+            nc.scalar.activation(
+                out=tile[:], in_=sum_bank[s][:, P : 2 * P], func=ACT.Copy, scale=e_inv[:, s : s + 1]
+            )
 
-        def project(s, ls):
-            g, t = s // 4, s % 4
-            for l in ls:
-                nc.vector.scalar_tensor_tensor(
-                    out=xb[g][:, t, l, :],
-                    in0=rr[s][:],
-                    scalar=mt[:, s, l : l + 1],
-                    in1=vcols(s, l),
-                    op0=ALU.mult,
-                    op1=ALU.add,
+        def project(s, l):
+            g, t = s // T, s % T
+            nc.vector.scalar_tensor_tensor(
+                out=x_flat[g][:, t, l, :],
+                in0=r_col[s][:],
+                scalar=m_col[:, s, l : l + 1],
+                in1=v_frame(s, l),
+                op0=ALU.mult,
+                op1=ALU.add,
+            )
+
+        def runs(view):
+            return view.rearrange("p (c i) t -> p c t i", i=4)
+
+        def interleave(g, j, engine):
+            target = x_word[g][:, 2 * j : 2 * j + 2, :, :].rearrange("p l b t -> p (l b) t")
+            source = x_flat[g][:, :, 2 * j : 2 * j + 2, :].rearrange("p t l b -> p (l b) t")
+            if engine == "gpsimd":
+                nc.gpsimd.tensor_scalar(
+                    out=target, in0=source, scalar1=1.0, scalar2=0.0, op0=ALU.mult, op1=ALU.add
                 )
-
-        def interleave(g, j, on_scalar):
-            dst = xi[g][:, 2 * j : 2 * j + 2, :, :].rearrange("p l b t -> p (l b) t")
-            src = xb[g][:, :, 2 * j : 2 * j + 2, :].rearrange("p t l b -> p (l b) t")
-            if on_scalar:
-                nc.scalar.copy(out=dst, in_=src)
+            elif engine == "scalar":
+                nc.scalar.copy(out=runs(target), in_=runs(source))
             else:
-                nc.vector.tensor_copy(out=dst, in_=src)
+                nc.vector.tensor_copy(out=runs(target), in_=runs(source))
 
-        def quant_x(g, h):
-            cols = slice(512 * h, 512 * h + 512)
+        def quantise_x(g, h):
+            cols = slice(HALF * h, HALF * (h + 1))
             nc.vector.quantize_mx(
-                out=xq[g][:, cols].bitcast(E4M3X4),
-                scales=xs[g][:, cols],
-                in_=xi[g][:, 4 * h : 4 * h + 4, :, :].rearrange("p l b t -> p (l b t)"),
+                out=x_codes[g][:, cols].bitcast(E4M3X4),
+                scales=x_code_scales[g][:, cols],
+                in_=x_word[g][:, HF * h : HF * (h + 1), :, :].rearrange("p l b t -> p (l b t)"),
             )
 
-        at = {}
-        res = {}
+        a_bank = {}
+        parts = {}
+        out_bank = {}
 
-        def mm2(h, ft, g):
+        def multiply_w(h, j, g):
             if g == 0:
-                at[(h, ft)] = vbank(ft % 2)
+                a_bank[(h, j)] = product_bank(j % 2)
+            cols = slice(HALF * h, HALF * (h + 1))
             nc.tensor.matmul_mx(
-                out=at[(h, ft)][:],
-                lhsT=ww[:, g, 256 * ft : 256 * ft + 256].bitcast(E2M1X4),
-                lhsT_scale=ws[:, g, P * ft : P * ft + P],
-                rhs=xq[g][:, 512 * h : 512 * h + 512].bitcast(E4M3X4),
-                rhs_scale=xs[g][:, 512 * h : 512 * h + 512],
+                out=a_bank[(h, j)][:],
+                lhsT=w_in[:, g, 2 * P * j : 2 * P * (j + 1)].bitcast(E2M1X4),
+                lhsT_scale=w_in_scales[:, g, P * j : P * (j + 1)],
+                rhs=x_codes[g][:, cols].bitcast(E4M3X4),
+                rhs_scale=x_code_scales[g][:, cols],
                 start=(g == 0),
                 stop=(g == G - 1),
             )
 
-        def pos_part(h, ft):
-            p = wtile([P, 512], F32, "pos", 6)
-            nc.scalar.activation(out=p[:], in_=at[(h, ft)][:], func=ACT.Relu, bias=thn[:, ft : ft + 1])
-            res.setdefault((h, ft), []).append(p)
+        def threshold_scalar(h, j):
+            if (h, j) not in ON_VECTOR:
+                tile = rotating([P, HALF], F32, "above", 8)
+                nc.scalar.activation(
+                    out=tile[:], in_=a_bank[(h, j)][:], func=ACT.Relu, bias=thr_neg[:, j : j + 1]
+                )
+                parts[(h, j)] = [tile]
 
-        def neg_part(h, ft):
-            q = wtile([P, 512], F32, "neg", 6)
-            nc.vector.tensor_scalar(
-                out=q[:], in0=at[(h, ft)][:], scalar1=thp[:, ft : ft + 1], scalar2=0.0, op0=ALU.add, op1=ALU.min
-            )
-            res.setdefault((h, ft), []).append(q)
+        def threshold_vector(h, j):
+            bank = a_bank[(h, j)]
+            if (h, j) in ON_VECTOR:
+                low = rotating([P, HALF], F32, "low", 2)
+                nc.vector.tensor_scalar(
+                    out=low[:], in0=bank[:], scalar1=thr_neg[:, j : j + 1], scalar2=None, op0=ALU.min
+                )
+                tile = rotating([P, HALF], F32, "both", 2)
+                nc.vector.scalar_tensor_tensor(
+                    out=tile[:], in0=bank[:], scalar=thr_col[:, j : j + 1], in1=low[:], op0=ALU.max, op1=ALU.add
+                )
+                parts[(h, j)] = [tile]
+            else:
+                tile = rotating([P, HALF], F32, "below", 8)
+                nc.vector.tensor_scalar(
+                    out=tile[:],
+                    in0=bank[:],
+                    scalar1=thr_col[:, j : j + 1],
+                    scalar2=0.0,
+                    op0=ALU.add,
+                    op1=ALU.min,
+                )
+                parts[(h, j)].append(tile)
 
-        low = {}
-
-        def low_part(h, ft):
-            q = wtile([P, 512], F32, "low", 3)
-            nc.vector.tensor_scalar(
-                out=q[:], in0=at[(h, ft)][:], scalar1=thn[:, ft : ft + 1], scalar2=None, op0=ALU.min
-            )
-            low[(h, ft)] = q
-
-        def both_parts(h, ft):
-            o = wtile([P, 512], F32, "both", 6)
-            nc.vector.scalar_tensor_tensor(
-                out=o[:], in0=at[(h, ft)][:], scalar=thp[:, ft : ft + 1], in1=low[(h, ft)][:], op0=ALU.max, op1=ALU.add
-            )
-            res[(h, ft)] = [o]
-
-        def emit(h, i, on_scalar):
-            l = 4 * h + i
-            bank = tbank() if h == 0 else vbank(i % 2)
-            for ft in range(4):
-                parts = res[(h, ft)]
-                for n, part in enumerate(parts):
+        def turn_out(h, i):
+            bank = turn_bank() if h == 0 else product_bank(i % 2)
+            out_bank[(h, i)] = bank
+            for j in range(FT):
+                for k, part in enumerate(parts[(h, j)]):
                     nc.tensor.matmul(
-                        out=bank[:, P * ft : P * ft + P],
-                        lhsT=part[:, P * i : P * i + P],
+                        out=bank[:, P * j : P * (j + 1)],
+                        lhsT=part[:, B * i : B * (i + 1)],
                         rhs=ident[:],
-                        start=(n == 0),
-                        stop=(n == len(parts) - 1),
+                        start=(k == 0),
+                        stop=(k == len(parts[(h, j)]) - 1),
                         is_transpose=True,
                     )
-            o = wtile([P, F], F32, "o", 6)
+
+        def store(h, i, on_scalar):
+            rows = rotating([P, F], F32, "rows", 8)
             if on_scalar:
-                nc.scalar.copy(out=o[:], in_=bank[:])
+                nc.scalar.copy(out=rows[:], in_=out_bank[(h, i)][:])
             else:
-                nc.vector.tensor_copy(out=o[:], in_=bank[:])
-            nc.sync.dma_start(out=out[:, l, :], in_=o[:])
+                nc.vector.tensor_copy(out=rows[:], in_=out_bank[(h, i)][:])
+            nc.sync.dma_start(out=out[:, HF * h + i, :], in_=rows[:])
 
         with tc.manual_schedule(engines={ENG.PE, ENG.Activation, ENG.DVE}):
+            for i in range(WARM_UPS):
+                warm_up()
             for l in range(L):
-                widen(l, l % 2 == 0)
-            turn(0)
-            turn(1)
-            prep_m_turn()
-            regroup(0, False)
-            regroup(1, True)
-            turn(2)
-            turn(3)
-            quant_c(0)
+                widen(l, on_scalar=(l % 2 == 1))
+            turn_c(0)
+            turn_c(1)
+            warm_up()
+            turn_m()
+            gather_c(0, on_scalar=False)
+            turn_c(2)
+            turn_c(3)
+            gather_c(1, on_scalar=True)
+            quantise_c(0)
             sort_d(0)
-            quant_c(1)
-            mm1(0, 0)
-            regroup(2, True)
-            regroup(3, False)
-            quant_c(2)
-            prep_m()
-            quant_c(3)
-            mm1(0, 1)
-            mm1(1, 0)
-            mm1(1, 1)
-            sort_d(1)
+            quantise_c(1)
+            prepare_m()
+            multiply_d(0, 0)
+            multiply_d(1, 0)
+            gather_c(2, on_scalar=True)
+            gather_c(3, on_scalar=True)
+            quantise_c(2)
+            quantise_c(3)
+            multiply_d(0, 1)
+            multiply_d(1, 1)
+            prepare_thr()
 
-            lo, hi = range(0, 4), range(4, 8)
-            for i in range(SL):
-                weigh(i, range(0, 6))
-                if i > 0:
-                    turn_back(i - 1)
-                weigh(i, range(6, 8))
-                if i == 1:
-                    prep_thr()
-                if i == 5:
-                    interleave(0, 0, True)
-                if i == 6:
-                    interleave(0, 2, True)
-                if i > 0:
-                    scale_back(i - 1)
-                resid(i)
-                if i > 0:
-                    project(i - 1, lo)
-                    project(i - 1, hi)
-                for h in range(2):
-                    if 1 <= i and i + 1 < SL:
-                        mm1(i + 1, h)
-                if i == 4:
-                    interleave(0, 1, False)
-                if i == 6:
-                    quant_x(0, 0)
-            i = SL - 1
-            turn_back(i)
-            interleave(0, 3, False)
-            quant_x(0, 1)
-            scale_back(i)
-            for ft in range(4):
-                mm2(0, ft, 0)
-            for ft in range(2):
-                mm2(1, ft, 0)
-            project(i, lo)
-            interleave(1, 1, True)
-            interleave(1, 0, False)
-            project(i, hi)
-            quant_x(1, 0)
-            interleave(1, 3, True)
-            interleave(1, 2, False)
-            for ft in range(4):
-                mm2(0, ft, 1)
-            quant_x(1, 1)
-            low_part(0, 1)
-            pos_part(0, 0)
-            low_part(0, 3)
-            pos_part(0, 2)
-            both_parts(0, 1)
-            neg_part(0, 0)
-            both_parts(0, 3)
-            neg_part(0, 2)
-            for ft in range(2):
-                mm2(1, ft, 1)
-            for ft in range(2, 4):
-                mm2(1, ft, 0)
-                mm2(1, ft, 1)
-            for ft in range(4):
-                pos_part(1, ft)
-            for ft in range(4):
-                neg_part(1, ft)
-            for ft in range(4):
-                emit(0, ft, True)
-            for i in range(4):
-                emit(1, i, i % 2 == 1)
+            for s in range(S):
+                for l in range(L):
+                    weigh(s, l)
+                    if s > 0 and l == 2:
+                        turn_residual(s - 1)
+                    if 1 <= s < S - 1 and l % HF == HF - 1:
+                        multiply_d(s + 1, l // HF)
+                if s == 0:
+                    residual(s)
+                    sort_d(1)
+                else:
+                    scale_residual(s - 1)
+                    for l in range(L):
+                        if l == 3:
+                            residual(s)
+                        project(s - 1, l)
+                if s >= T:
+                    interleave(0, s - T, "gpsimd" if s < S - 1 else "scalar")
+            quantise_x(0, 0)
+            s = S - 1
+            turn_residual(s)
+            for j in range(FT):
+                multiply_w(0, j, 0)
+            scale_residual(s)
+            for l in range(HF):
+                project(s, l)
+            interleave(1, 1, "scalar")
+            for l in range(HF, L):
+                project(s, l)
+            interleave(1, 0, "vector")
+            interleave(1, 2, "vector")
+            quantise_x(1, 0)
+            quantise_x(0, 1)
+            interleave(1, 3, "scalar")
+            for j in range(FT):
+                multiply_w(0, j, 1)
+            for j in range(FT):
+                threshold_scalar(0, j)
+            quantise_x(1, 1)
+            for j in range(FT):
+                threshold_vector(0, j)
+            for j in range(FT):
+                multiply_w(1, j, 0)
+                multiply_w(1, j, 1)
+                threshold_scalar(1, j)
+            for j in range(FT):
+                threshold_vector(1, j)
+            for i in range(HF):
+                turn_out(0, i)
+                store(0, i, on_scalar=(i < HF - 1))
+            for i in range(HF):
+                turn_out(1, i)
+                store(1, i, on_scalar=(i % 2 == 1))

from contextlib import ExitStack

import concourse.mybir as mybir
from concourse.masks import make_identity

B, L, K, N, F = 128, 8, 512, 1024, 512
FLOPS = 2 * B * L * (K * N + N * F)

P = 128
T = 4
G = N // (P * T)
S = N // P
FT = F // P
HF = L // 2
HALF = HF * B

F32 = mybir.dt.float32
BF16 = mybir.dt.bfloat16
I32 = mybir.dt.int32
U32 = mybir.dt.uint32
U8 = mybir.dt.uint8
FP8 = mybir.dt.float8_e4m3fn
E4M3X4 = mybir.dt.float8_e4m3fn_x4
E2M1X4 = mybir.dt.float4_e2m1fn_x4

ALU = mybir.AluOpType
ACT = mybir.ActivationFunctionType
ENG = mybir.EngineType

LOAD_FRAMES = (2, 2, 4)

ON_VECTOR = ((0, 0), (1, 2))

WARM_UPS = 7


def tile_snapshotcompressivegapprojectiondictiona_d1p_kernel(
    tc, c_bytes, c_scale, d_words, d_scales, m, y, w_words, w_scales, thr, out
):
    nc = tc.nc
    with ExitStack() as ctx:
        keep = ctx.enter_context(tc.tile_pool(name="keep", bufs=1))
        work = ctx.enter_context(tc.tile_pool(name="work", bufs=1))
        psum = ctx.enter_context(tc.psum_pool(name="psum", bufs=1))

        def kept(shape, dtype, name):
            return keep.tile(shape, dtype, name=name, tag=name, align_bytes=64)

        def rotating(shape, dtype, name, bufs):
            return work.tile(shape, dtype, name=name, tag=name, bufs=bufs, align_bytes=64)

        def product_bank(h):
            return psum.tile([P, HALF], F32, name="product%d" % h, tag="product%d" % h, bufs=3)

        def turn_bank():
            return psum.tile([P, 512], F32, name="turn", tag="turn", bufs=2)

        scale_c = kept([P, L * T], F32, "scale_c")
        bytes_c = [kept([P, frames, K], U8, "bytes_c%d" % j) for j, frames in enumerate(LOAD_FRAMES)]
        d_in = kept([P, 2 * N], U8, "d_in")
        d_in_scales = kept([P, N], U8, "d_in_scales")
        w_in = kept([P, G, 2 * F], U8, "w_in")
        w_in_scales = kept([P, G, F], U8, "w_in_scales")
        m_rows = kept([P, N], BF16, "m_rows")
        thr_rows = kept([P, P], BF16, "thr_rows")
        y_in = kept([P, N], BF16, "y_in")
        ident = kept([P, P], F32, "ident")
        blank = kept([P, 512], BF16, "blank")

        nc.vector.memset(d_in_scales[:].bitcast(I32), 0)
        nc.vector.memset(m_rows[:].bitcast(I32), 0)
        nc.vector.memset(thr_rows[:].bitcast(I32), 0)
        nc.vector.memset(w_in_scales[:].rearrange("p g f -> p (g f)").bitcast(I32), 0)
        make_identity(nc, ident[:])
        nc.vector.memset(blank[:].bitcast(I32), 0)

        nc.sync.dma_start(out=scale_c[:], in_=c_scale.rearrange("b l j -> b (l j)"))
        source_c = {}
        first = 0
        for j, frames in enumerate(LOAD_FRAMES):
            nc.sync.dma_start(out=bytes_c[j][:], in_=c_bytes[:, first : first + frames, :])
            for i in range(frames):
                source_c[first + i] = (bytes_c[j], i)
            first += frames
        nc.scalar.dma_start(out=d_in[:].bitcast(I32), in_=d_words[0].bitcast(I32))
        for q in range(4):
            nc.scalar.dma_start(
                out=d_in_scales[32 * q : 32 * q + 4, :].bitcast(I32),
                in_=d_scales[0, 4 * q : 4 * q + 4, :].bitcast(I32),
            )
        nc.gpsimd.dma_start(out=m_rows[0:L, :], in_=m)
        nc.gpsimd.dma_start(out=thr_rows[0:FT, :], in_=thr.rearrange("(j q) -> j q", q=P))
        nc.sync.dma_start(out=y_in[:], in_=y)
        for q in range(4):
            nc.sync.dma_start(
                out=w_in_scales[32 * q : 32 * q + 4, :, :].bitcast(I32),
                in_=w_scales[:, 4 * q : 4 * q + 4, :].rearrange("g q n -> q g n").bitcast(I32),
            )
        for g in range(G):
            nc.sync.dma_start(out=w_in[:, g, :].bitcast(I32), in_=w_words[g].bitcast(I32))

        d_codes = kept([P, 2 * N], U8, "d_codes")
        d_code_scales = kept([P, N], U8, "d_code_scales")
        c_codes = kept([P, B * L], U32, "c_codes")
        c_code_scales = kept([P, B * L], U8, "c_code_scales")
        m_col = kept([P, S, L], F32, "m_col")
        m_sq = kept([P, S, L], F32, "m_sq")
        e_sum = kept([P, S], F32, "e_sum")
        e_inv = kept([P, S], F32, "e_inv")
        thr_f32 = kept([P, P], F32, "thr_f32")
        thr_col = kept([P, FT], F32, "thr_col")
        thr_neg = kept([P, FT], F32, "thr_neg")
        x_flat = [kept([P, T, L, B], BF16, "x_flat%d" % g) for g in range(G)]
        x_word = [kept([P, L, B, T], BF16, "x_word%d" % g) for g in range(G)]
        x_codes = [kept([P, B * L], U32, "x_codes%d" % g) for g in range(G)]
        x_code_scales = [kept([P, B * L], U8, "x_code_scales%d" % g) for g in range(G)]

        def warm_up():
            bank = product_bank(0)
            nc.tensor.matmul(out=bank[:], lhsT=blank[:, 0:P], rhs=blank[:], start=True, stop=True)

        c_rows = {}
        c_turned = {}
        c_word = {}

        def widen(l, on_scalar):
            rows = rotating([P, K], BF16, "c_rows", 8)
            c_rows[l] = rows
            tile, i = source_c[l]
            for j in range(T):
                source = tile[:, i, P * j : P * j + P].bitcast(FP8)
                scale = scale_c[:, T * l + j : T * l + j + 1]
                target = rows[:, P * j : P * j + P]
                if on_scalar:
                    nc.scalar.activation(out=target, in_=source, func=ACT.Copy, scale=scale)
                else:
                    nc.vector.tensor_scalar(out=target, in0=source, scalar1=scale, scalar2=None, op0=ALU.mult)

        def turn_c(j):
            bank = product_bank(j % 2)
            c_turned[j] = bank
            for i in range(2):
                words = c_rows[2 * j + i][:].bitcast(F32)
                for u in range(2):
                    first = 2 * P * i + P * u
                    nc.tensor.transpose(bank[:, first : first + P], words[:, u::2], ident[:])

        def gather_c(j, on_scalar):
            tile = rotating([P, 2 * B * T], BF16, "c_word", 4)
            c_word[j] = tile
            target = tile[:].bitcast(F32).rearrange("p (l b u) -> p l b u", l=2, u=2)
            source = c_turned[j][:].rearrange("p (l u b) -> p l b u", l=2, u=2)
            if on_scalar:
                nc.scalar.copy(out=target, in_=source)
            else:
                nc.vector.tensor_copy(out=target, in_=source)

        def quantise_c(j):
            cols = slice(2 * B * j, 2 * B * (j + 1))
            nc.vector.quantize_mx(
                out=c_codes[:, cols].bitcast(E4M3X4), scales=c_code_scales[:, cols], in_=c_word[j][:]
            )

        def sort_d(g):
            words = slice(1024 * g, 1024 * (g + 1))
            nc.vector.tensor_copy(
                out=d_codes[:, words].rearrange("p (t q i) -> p t q i", t=T, i=2),
                in_=d_in[:, words].rearrange("p (q t i) -> p t q i", t=T, i=2),
            )
            cols = slice(512 * g, 512 * (g + 1))
            nc.vector.tensor_copy(
                out=d_code_scales[:, cols].rearrange("p (t q) -> p t q", t=T),
                in_=d_in_scales[:, cols].rearrange("p (q t) -> p t q", t=T),
            )

        m_turned = {}

        def turn_m():
            bank = turn_bank()
            m_turned[0] = bank
            words = m_rows[:].bitcast(F32)
            for g in range(G):
                for u in range(2):
                    first = P * (2 * g + u)
                    nc.tensor.transpose(
                        bank[:, first : first + P], words[:, 256 * g + u : 256 * (g + 1) : 2], ident[:]
                    )

        def prepare_m():
            source = m_turned[0][:].bitcast(BF16).rearrange("p (k c e) -> p k e c", k=4, e=2)[:, :, :, 0:L]
            nc.vector.tensor_copy(out=m_col[:].rearrange("p (k e) l -> p k e l", e=2), in_=source)
            nc.vector.tensor_mul(out=m_sq[:], in0=m_col[:], in1=m_col[:])
            nc.vector.tensor_reduce(out=e_sum[:], in_=m_sq[:], axis=mybir.AxisListType.X, op=ALU.add)
            nc.vector.reciprocal(out=e_inv[:], in_=e_sum[:])

        def prepare_thr():
            nc.vector.tensor_copy(out=thr_f32[:], in_=thr_rows[:])
            bank = turn_bank()
            nc.tensor.transpose(bank[:, 0:P], thr_f32[:], ident[:])
            nc.vector.tensor_copy(out=thr_col[:], in_=bank[:, 0:FT])
            nc.vector.tensor_scalar(out=thr_neg[:], in0=thr_col[:], scalar1=-1.0, scalar2=None, op0=ALU.mult)

        v_bank = {}
        weighted = {}
        sum_bank = {}
        r_rows = {}
        r_col = {}

        def multiply_d(s, h):
            bank = product_bank(h)
            v_bank[(s, h)] = bank
            cols = slice(HALF * h, HALF * (h + 1))
            nc.tensor.matmul_mx(
                out=bank[:],
                lhsT=d_codes[:, 2 * P * s : 2 * P * (s + 1)].bitcast(E2M1X4),
                lhsT_scale=d_code_scales[:, P * s : P * (s + 1)],
                rhs=c_codes[:, cols].bitcast(E4M3X4),
                rhs_scale=c_code_scales[:, cols],
                start=True,
                stop=True,
            )

        def v_frame(s, l):
            first = B * (l % HF)
            return v_bank[(s, l // HF)][:, first : first + B]

        def weigh(s, l):
            tile = rotating([P, B], F32, "weighted", 16)
            nc.scalar.activation(out=tile[:], in_=v_frame(s, l), func=ACT.Copy, scale=m_col[:, s, l : l + 1])
            if l == 0:
                sum_bank[s] = turn_bank()
            nc.tensor.matmul(
                out=sum_bank[s][:, 0:P],
                lhsT=tile[:],
                rhs=ident[:],
                start=(l == 0),
                stop=(l == L - 1),
                is_transpose=True,
            )

        def residual(s):
            g, t = s // T, s % T
            tile = rotating([P, P], F32, "r_rows", 2)
            r_rows[s] = tile
            nc.vector.tensor_tensor(
                out=tile[:],
                in0=y_in[:, 512 * g + t : 512 * (g + 1) : T],
                in1=sum_bank[s][:, 0:P],
                op=ALU.subtract,
            )

        def turn_residual(s):
            nc.tensor.transpose(sum_bank[s][:, P : 2 * P], r_rows[s][:], ident[:])

        def scale_residual(s):
            tile = rotating([P, B], F32, "r_col", 6)
            r_col[s] = tile
            nc.scalar.activation(
                out=tile[:], in_=sum_bank[s][:, P : 2 * P], func=ACT.Copy, scale=e_inv[:, s : s + 1]
            )

        def project(s, l):
            g, t = s // T, s % T
            nc.vector.scalar_tensor_tensor(
                out=x_flat[g][:, t, l, :],
                in0=r_col[s][:],
                scalar=m_col[:, s, l : l + 1],
                in1=v_frame(s, l),
                op0=ALU.mult,
                op1=ALU.add,
            )

        def runs(view):
            return view.rearrange("p (c i) t -> p c t i", i=4)

        def interleave(g, j, engine):
            target = x_word[g][:, 2 * j : 2 * j + 2, :, :].rearrange("p l b t -> p (l b) t")
            source = x_flat[g][:, :, 2 * j : 2 * j + 2, :].rearrange("p t l b -> p (l b) t")
            if engine == "gpsimd":
                nc.gpsimd.tensor_scalar(
                    out=target, in0=source, scalar1=1.0, scalar2=0.0, op0=ALU.mult, op1=ALU.add
                )
            elif engine == "scalar":
                nc.scalar.copy(out=runs(target), in_=runs(source))
            else:
                nc.vector.tensor_copy(out=runs(target), in_=runs(source))

        def quantise_x(g, h):
            cols = slice(HALF * h, HALF * (h + 1))
            nc.vector.quantize_mx(
                out=x_codes[g][:, cols].bitcast(E4M3X4),
                scales=x_code_scales[g][:, cols],
                in_=x_word[g][:, HF * h : HF * (h + 1), :, :].rearrange("p l b t -> p (l b t)"),
            )

        a_bank = {}
        parts = {}
        out_bank = {}

        def multiply_w(h, j, g):
            if g == 0:
                a_bank[(h, j)] = product_bank(j % 2)
            cols = slice(HALF * h, HALF * (h + 1))
            nc.tensor.matmul_mx(
                out=a_bank[(h, j)][:],
                lhsT=w_in[:, g, 2 * P * j : 2 * P * (j + 1)].bitcast(E2M1X4),
                lhsT_scale=w_in_scales[:, g, P * j : P * (j + 1)],
                rhs=x_codes[g][:, cols].bitcast(E4M3X4),
                rhs_scale=x_code_scales[g][:, cols],
                start=(g == 0),
                stop=(g == G - 1),
            )

        def threshold_scalar(h, j):
            if (h, j) not in ON_VECTOR:
                tile = rotating([P, HALF], F32, "above", 8)
                nc.scalar.activation(
                    out=tile[:], in_=a_bank[(h, j)][:], func=ACT.Relu, bias=thr_neg[:, j : j + 1]
                )
                parts[(h, j)] = [tile]

        def threshold_vector(h, j):
            bank = a_bank[(h, j)]
            if (h, j) in ON_VECTOR:
                low = rotating([P, HALF], F32, "low", 2)
                nc.vector.tensor_scalar(
                    out=low[:], in0=bank[:], scalar1=thr_neg[:, j : j + 1], scalar2=None, op0=ALU.min
                )
                tile = rotating([P, HALF], F32, "both", 2)
                nc.vector.scalar_tensor_tensor(
                    out=tile[:], in0=bank[:], scalar=thr_col[:, j : j + 1], in1=low[:], op0=ALU.max, op1=ALU.add
                )
                parts[(h, j)] = [tile]
            else:
                tile = rotating([P, HALF], F32, "below", 8)
                nc.vector.tensor_scalar(
                    out=tile[:],
                    in0=bank[:],
                    scalar1=thr_col[:, j : j + 1],
                    scalar2=0.0,
                    op0=ALU.add,
                    op1=ALU.min,
                )
                parts[(h, j)].append(tile)

        def turn_out(h, i):
            bank = turn_bank() if h == 0 else product_bank(i % 2)
            out_bank[(h, i)] = bank
            for j in range(FT):
                for k, part in enumerate(parts[(h, j)]):
                    nc.tensor.matmul(
                        out=bank[:, P * j : P * (j + 1)],
                        lhsT=part[:, B * i : B * (i + 1)],
                        rhs=ident[:],
                        start=(k == 0),
                        stop=(k == len(parts[(h, j)]) - 1),
                        is_transpose=True,
                    )

        def store(h, i, on_scalar):
            rows = rotating([P, F], F32, "rows", 8)
            if on_scalar:
                nc.scalar.copy(out=rows[:], in_=out_bank[(h, i)][:])
            else:
                nc.vector.tensor_copy(out=rows[:], in_=out_bank[(h, i)][:])
            nc.sync.dma_start(out=out[:, HF * h + i, :], in_=rows[:])

        with tc.manual_schedule(engines={ENG.PE, ENG.Activation, ENG.DVE}):
            for i in range(WARM_UPS):
                warm_up()
            for l in range(L):
                widen(l, on_scalar=(l % 2 == 1))
            turn_c(0)
            turn_c(1)
            warm_up()
            turn_m()
            gather_c(0, on_scalar=False)
            turn_c(2)
            turn_c(3)
            gather_c(1, on_scalar=True)
            quantise_c(0)
            sort_d(0)
            quantise_c(1)
            prepare_m()
            multiply_d(0, 0)
            multiply_d(1, 0)
            gather_c(2, on_scalar=True)
            gather_c(3, on_scalar=True)
            quantise_c(2)
            quantise_c(3)
            multiply_d(0, 1)
            multiply_d(1, 1)
            prepare_thr()

            for s in range(S):
                for l in range(L):
                    weigh(s, l)
                    if s > 0 and l == 2:
                        turn_residual(s - 1)
                    if 1 <= s < S - 1 and l % HF == HF - 1:
                        multiply_d(s + 1, l // HF)
                if s == 0:
                    residual(s)
                    sort_d(1)
                else:
                    scale_residual(s - 1)
                    for l in range(L):
                        if l == 3:
                            residual(s)
                        project(s - 1, l)
                if s >= T:
                    interleave(0, s - T, "gpsimd" if s < S - 1 else "scalar")
            quantise_x(0, 0)
            s = S - 1
            turn_residual(s)
            for j in range(FT):
                multiply_w(0, j, 0)
            scale_residual(s)
            for l in range(HF):
                project(s, l)
            interleave(1, 1, "scalar")
            for l in range(HF, L):
                project(s, l)
            interleave(1, 0, "vector")
            interleave(1, 2, "vector")
            quantise_x(1, 0)
            quantise_x(0, 1)
            interleave(1, 3, "scalar")
            for j in range(FT):
                multiply_w(0, j, 1)
            for j in range(FT):
                threshold_scalar(0, j)
            quantise_x(1, 1)
            for j in range(FT):
                threshold_vector(0, j)
            for j in range(FT):
                multiply_w(1, j, 0)
                multiply_w(1, j, 1)
                threshold_scalar(1, j)
            for j in range(FT):
                threshold_vector(1, j)
            for i in range(HF):
                turn_out(0, i)
                store(0, i, on_scalar=(i < HF - 1))
            for i in range(HF):
                turn_out(1, i)
                store(1, i, on_scalar=(i % 2 == 1))
